import numpy as np
import ml_dtypes


def mxq(x, axis, fmt="e4m3"):
    dtype, down = {"e4m3": (ml_dtypes.float8_e4m3fn, 7), "e5m2": (ml_dtypes.float8_e5m2, 14)}[fmt]
    v = np.moveaxis(np.asarray(x, np.float32).astype(ml_dtypes.bfloat16).astype(np.float64), axis, -1)
    blocks = v.reshape(v.shape[:-1] + (-1, 32))
    amax = np.abs(blocks).max(-1, keepdims=True)
    byte = np.maximum(np.where(amax > 0, np.frexp(amax)[1] - 1 + 127, 0) - down, 1)
    scale = np.exp2(byte - 127.0)
    codes = (blocks / scale).astype(np.float32).astype(dtype).astype(np.float64)
    return np.moveaxis((codes * scale).reshape(v.shape), -1, axis)


WIDE = False


def mx_kscale(k):
    if not WIDE:
        return np.ones(k)
    levels = np.array([30, -30])
    if k % 512:
        return np.exp2(np.random.permutation(np.resize(levels, k // 32))).repeat(32)
    a = np.empty((k // 512, 16))
    for p in range(k // 512):
        a[p, :8] = np.random.permutation(np.resize(levels, 8))
        for g in range(8):
            far = levels[np.abs(levels - a[p, g]) >= 10]
            a[p, g + 8] = far[np.random.randint(len(far))]
    return np.exp2(a.ravel()).repeat(32)


BF16 = ml_dtypes.bfloat16


def bf(x):
    return np.asarray(x, np.float32).astype(BF16)


def f64(x):
    return np.asarray(x).astype(np.float64)


E2M1 = np.array([0.0, 0.5, 1.0, 1.5, 2.0, 3.0, 4.0, 6.0, -0.0, -0.5, -1.0, -1.5, -2.0, -3.0, -4.0, -6.0])


def pack_weight(w, fmt):
    k, n = w.shape
    w = f64(bf(w)).reshape(k // 32, 32, n)
    amax = np.abs(w).max(1)
    if fmt == "e4m3":
        byte = np.frexp(amax)[1] - 1 + 127 - 7
    else:
        mant, ex = np.frexp(amax / 6.0)
        byte = np.where(mant > 0.5, ex, ex - 1) + 127
    byte = np.clip(np.where(amax > 0, byte, 1), 1, 254)
    scaled = (w * np.exp2(127.0 - byte)[:, None, :]).reshape(k, n).astype(np.float32)
    by_word = np.ascontiguousarray(scaled.reshape(k // 512, 128, 4, n).transpose(0, 1, 3, 2))
    if fmt == "e4m3":
        words = by_word.astype(ml_dtypes.float8_e4m3fn).view(np.uint8)
    else:
        c = by_word.astype(ml_dtypes.float4_e2m1fn).view(np.uint8) & 0xF
        words = c[..., 0::2] | (c[..., 1::2] << 4)
    return np.ascontiguousarray(words), np.ascontiguousarray(byte.astype(np.uint8).reshape(k // 512, 16, n))


def unpack_weight(words, scales, fmt):
    g, p, n, _ = words.shape
    if fmt == "e4m3":
        vals = np.ascontiguousarray(words).view(ml_dtypes.float8_e4m3fn).astype(np.float64)
    else:
        nib = np.empty((g, p, n, 4), np.uint8)
        nib[..., 0::2] = words & 0xF
        nib[..., 1::2] = words >> 4
        vals = E2M1[nib]
    vals = vals * np.repeat(np.exp2(scales.astype(np.float64) - 127.0), 8, axis=1)[..., None]
    return vals.transpose(0, 1, 3, 2).reshape(g * 512, n)
def pack4(w):
    words, scales = pack_weight(w, "e2m1")
    return words.reshape(words.shape[0], 128, -1), scales


def unpack4(words, scales):
    return unpack_weight(words.reshape(words.shape[0], 128, -1, 2), scales, "e2m1")


T, C, G, P, D = 2, 1024, 1536, 1024, 512


def setup_inputs():
    s, t = mx_kscale(G), mx_kscale(C)
    mix = np.random.standard_normal((G, P)) / np.sqrt(G) / s[:, None]
    mix_words, mix_scales = pack4(mix)
    return {"x": bf(np.random.standard_normal((T, C, G)) * s),
            "mix_words": mix_words,
            "mix_scales": mix_scales,
            "surface": bf(0.5 * np.random.standard_normal((C, P))),
            "gain": bf((1 + 0.1 * np.random.standard_normal((T, C))) * t),
            "w": bf(np.random.standard_normal((C, D)) / np.sqrt(C) / t[:, None]),
            "b": bf(0.3 * np.random.standard_normal(D))}


def reference(x, mix_words, mix_scales, surface, gain, w, b):
    xq = mxq(f64(x), 2, "e4m3").reshape(T * C, G)
    mixed = (xq @ unpack4(mix_words, mix_scales)).reshape(T, C, P)
    h = np.maximum(mixed + f64(surface), 0) * f64(gain)[:, :, None]
    hq = mxq(h, 1, "e5m2").transpose(1, 0, 2).reshape(C, T * P)
    wq = mxq(f64(w), 0, "e4m3")
    y = (wq.T @ hq) + f64(b)[:, None]
    return y.reshape(D, T, P).transpose(1, 0, 2)

from contextlib import ExitStack

import concourse.mybir as mybir
from concourse.masks import make_identity

T, C, G, M, D = 2, 1024, 1536, 1024, 512
FLOPS = 2 * T * C * G * M + 2 * T * C * M * D

F32 = mybir.dt.float32
BF16 = mybir.dt.bfloat16
I32 = mybir.dt.int32
U32 = mybir.dt.uint32
U8 = mybir.dt.uint8
E4M3 = mybir.dt.float8_e4m3fn_x4
E5M2 = mybir.dt.float8_e5m2_x4
E2M1 = mybir.dt.float4_e2m1fn_x4
ALU = mybir.AluOpType
ACT = mybir.ActivationFunctionType

P = 128
NH = 512


PARAMS = {'units': ((0, 0, 0), (0, 0, 1), (0, 1, 0), (0, 1, 1), (1, 0, 0), (1, 1, 0), (1, 0, 1), (1, 1, 1)), 'lag': {'XC': 0, 'XQ': 1, 'A': 2, 'B': 3, 'C': 2, 'Q': 4, 'OUT': 4, 'W': 18}, 'prio': {'XC': -1, 'XQ': 2, 'A': -1, 'B': -1, 'C': 2, 'Q': 1, 'OUT': 0, 'W': -2}, 'xrun': {(1, 0): 4, (2, 1): 5, (3, 0): 4, (4, 0): 5}, 'mm2': {(5, 0): ((0, 0, 0), (0, 0, 1)), (5, 2): ((0, 0, 2),), (6, 0): ((0, 0, 3),), (6, 3): ((0, 1, 0), (0, 1, 1)), (7, 2): ((0, 1, 2),), (7, 3): ((0, 1, 3), (1, 0, 0), (1, 0, 1), (1, 0, 2), (1, 0, 3))}, 'tailplan': (('p', 0), ('p', 1), ('p', 2), ('p', 3), ('w',), ('e', 0, 'S'), ('e', 1, 'V'), ('e', 2, 'S'), ('e', 3, 'V')), 'headv': 1, 'cparts': 2, 'wslot': 8, 'tailc': 128, 'stt': (), 'nbank': 8}


def tile_weather_grid_channel_mixing_s9_kernel(tc, x, mix_words, mix_scales, surface, gain, w, b, out):
    nc = tc.nc
    pr = PARAMS
    units = pr["units"]
    with ExitStack() as ctx:
        keep = ctx.enter_context(tc.tile_pool(name="keep", bufs=1))
        work = ctx.enter_context(tc.tile_pool(name="work", bufs=2))
        psum = ctx.enter_context(tc.psum_pool(name="psum", bufs=pr["nbank"]))
        ctx.enter_context(tc.manual_schedule())

        warm = keep.tile([P, 1], F32, name="warm")
        nc.vector.memset(warm[:], 0.0)
        a_scales = keep.tile([P, 3, M], U8, align_bytes=64, name="a_scales")
        nc.vector.memset(a_scales[:].rearrange("p g n -> p (g n)").bitcast(I32), 0)
        warm2 = keep.tile([P, 1], F32, name="warm2")
        nc.scalar.activation(out=warm2[:], in_=warm[:], func=ACT.Identity, bias=0.0, scale=1.0)
        ident = keep.tile([P, P], F32, name="ident")
        make_identity(nc, ident[:])

        x_raw = {(a, g): keep.tile([P, 4, G], BF16, align_bytes=64, name=f"x_raw_{a}_{g}") for a in range(T) for g in range(2)}
        a_words = [keep.tile([P, 3, 2 * NH], U8, align_bytes=64, name=f"a_words_{h}") for h in range(2)]
        surf = [keep.tile([P, 4, M], BF16, align_bytes=64, name=f"surf_{g}") for g in range(2)]
        gain_bf = keep.tile([P, 4, 4], BF16, name="gain_bf")
        gain_sb = keep.tile([P, 4, 4], F32, name="gain_sb")
        b_sb = keep.tile([P, 4], BF16, name="b_sb")
        w_raw = keep.tile([P, 2, 4, D], BF16, align_bytes=64, name="w_raw")

        def load_x(a, g, t0, t1):
            nc.sync.dma_start(
                out=x_raw[a, g][:, t0:t1, :],
                in_=x[a, 512 * g : 512 * (g + 1), :].rearrange("(p t) r -> p t r", t=4)[:, t0:t1, :],
            )

        def load_words(h):
            nc.sync.dma_start(
                out=a_words[h][:].bitcast(I32),
                in_=mix_words.rearrange("g p n -> p g n")[:, :, 2 * NH * h : 2 * NH * (h + 1)].bitcast(I32),
            )

        def load_surf(g, t0, t1):
            nc.sync.dma_start(
                out=surf[g][:, t0:t1, :],
                in_=surface[512 * g : 512 * (g + 1), :].rearrange("(p t) m -> p t m", t=4)[:, t0:t1, :],
            )

        load_x(0, 0, 0, 1)
        load_x(0, 0, 1, 2)
        for q in range(4):
            nc.sync.dma_start(
                out=a_scales[32 * q : 32 * q + 4, :, :].bitcast(I32),
                in_=mix_scales[:, 4 * q : 4 * q + 4, :].rearrange("g r n -> r g n").bitcast(I32),
            )
        load_words(0)
        load_x(0, 0, 2, 3)
        load_x(0, 0, 3, 4)
        nc.sync.dma_start(out=gain_bf[:], in_=gain.rearrange("a (g p t) -> p (a g) t", g=2, t=4))
        load_surf(0, 0, 2)
        load_surf(0, 2, 4)
        load_words(1)
        load_x(0, 1, 0, 2)
        load_x(0, 1, 2, 4)
        load_surf(1, 0, 4)
        nc.sync.dma_start(out=b_sb[:], in_=b.rearrange("(p j) -> p j", j=4))
        nc.sync.dma_start(out=w_raw[:], in_=w.rearrange("(g p t) d -> p g t d", g=2, t=4))
        for g in range(2):
            load_x(1, g, 0, 2)
            load_x(1, g, 2, 4)

        pending = []
        clock = {"slot": 0, "n": 0}

        def later(kind, extra, fn):
            clock["n"] += 1
            pending.append((clock["slot"] + pr["lag"][kind] + extra, pr["prio"][kind], clock["n"], fn))

        def tick():
            while True:
                due = [e for e in pending if e[0] <= clock["slot"]]
                if not due:
                    break
                due.sort(key=lambda e: (e[0], e[1], e[2]))
                pending.remove(due[0])
                due[0][3]()
            clock["slot"] += 1

        x_codes, x_scales, grouped = {}, {}, {}

        def x_bank(a, g, n):
            words = x_raw[a, g][:].bitcast(F32)
            bank = psum.tile([P, 2, 2, P], F32, name="bank")
            for i in range(2):
                t, j = divmod(2 * n + i, 3)
                for u in range(2):
                    nc.tensor.transpose(bank[:, i, u, :], words[:, t, 256 * j + u : 256 * (j + 1) : 2], ident[:])
            if n % 2 == 0:
                grouped[a, g, n // 2] = work.tile([P, 4, P, 4], BF16, align_bytes=64, name="grouped", bufs=3)
            gt = grouped[a, g, n // 2]

            def copy():
                dst = gt[:, 2 * (n % 2) : 2 * (n % 2) + 2, :, :].bitcast(F32)
                src = bank[:].rearrange("p t u r -> p t r u")
                if (a, g) == (0, 0) and n % 2 == pr["headv"]:
                    nc.vector.tensor_copy(out=dst, in_=src)
                else:
                    nc.scalar.copy(out=dst, in_=src)
                if n % 2:
                    later("XQ", 0, quant)

            def quant():
                xc = keep.tile([P, 4 * P], U32, align_bytes=64, name=f"x_codes_{a}_{g}_{n // 2}")
                xs = keep.tile([P, 4 * P], U8, align_bytes=64, name=f"x_scales_{a}_{g}_{n // 2}")
                nc.vector.quantize_mx(out=xc[:].bitcast(E4M3), scales=xs[:], in_=gt[:].rearrange("p t r k -> p (t r k)"))
                x_codes[a, g, n // 2], x_scales[a, g, n // 2] = xc, xs

            later("XC", 0, copy)

        h_codes, h_scales, zt, hbt = {}, {}, {}, {}

        def mm1(i, t):
            a, g, h = units[i]
            acc = psum.tile([P, NH], F32, name="acc", tag="bank")
            for j in range(3):
                q, r = divmod(3 * t + j, 4)
                nc.tensor.matmul_mx(
                    out=acc[:],
                    lhsT=x_codes[a, g, q][:, P * r : P * (r + 1)].bitcast(E4M3),
                    lhsT_scale=x_scales[a, g, q][:, P * r : P * (r + 1)],
                    rhs=a_words[h][:, j, :].bitcast(E2M1),
                    rhs_scale=a_scales[:, j, NH * h : NH * (h + 1)],
                    start=(j == 0),
                    stop=(j == 2),
                )
            if t == 0:
                zt[i] = work.tile([P, 4, NH], F32, align_bytes=64, name="z")
                if i not in pr["stt"]:
                    hbt[i] = work.tile([P, 4, NH], BF16, align_bytes=64, name="hb")

            def add():
                nc.vector.tensor_tensor(out=zt[i][:, t, :], in0=acc[:], in1=surf[g][:, t, NH * h : NH * (h + 1)], op=ALU.add)
                if i not in pr["stt"]:
                    later("B", 0, gate)
                elif t == 3:
                    later("C", 0, inter)

            def gate():
                nc.vector.tensor_scalar(
                    out=hbt[i][:, t, :], in0=zt[i][:, t, :], scalar1=0.0, scalar2=gain_sb[:, 2 * a + g, t : t + 1], op0=ALU.max, op1=ALU.mult
                )
                if t == 3:
                    later("C", 0, inter)

            def inter():
                hi = work.tile([P, NH, 4], BF16, align_bytes=64, name="hi")
                if i in pr["stt"]:
                    for q in range(2):
                        lo, hi_ = 256 * q, 256 * (q + 1)
                        nc.vector.scalar_tensor_tensor(
                            out=hi[:, lo:hi_, :], in0=zt[i][:, :, lo:hi_].rearrange("p t m -> p m t"), scalar=0.0,
                            in1=gain_sb[:, 2 * a + g, :].unsqueeze(1).to_broadcast([P, 256, 4]), op0=ALU.max, op1=ALU.mult)
                else:
                    src = hbt[i][:].rearrange("p t m -> p m t")
                    if i == 7:
                        c = pr["tailc"]
                        nc.scalar.copy(out=hi[:, :c, :], in_=src[:, :c, :])
                        nc.vector.tensor_copy(out=hi[:, c:, :], in_=src[:, c:, :])
                    else:
                        n = NH // pr["cparts"]
                        for q in range(pr["cparts"]):
                            nc.scalar.copy(out=hi[:, n * q : n * (q + 1), :], in_=src[:, n * q : n * (q + 1), :])

                def quant():
                    hc = keep.tile([P, NH], U32, align_bytes=64, name=f"h_codes_{a}_{g}_{h}")
                    hs = keep.tile([P, NH], U8, align_bytes=64, name=f"h_scales_{a}_{g}_{h}")
                    nc.vector.quantize_mx(out=hc[:].bitcast(E5M2), scales=hs[:], in_=hi[:].rearrange("p m t -> p (m t)"))
                    h_codes[a, g, h], h_scales[a, g, h] = hc, hs

                later("Q", -pr["lag"]["Q"] if i == 7 else 0, quant)

            later("A", 0, add)

        w_codes, w_scales, wis = [], [], []

        def prep_w():
            for g in range(2):
                wi = work.tile([P, 4, P, 4], BF16, align_bytes=64, name="wi")
                nc.gpsimd.tensor_scalar(
                    out=wi[:], in0=w_raw[:, g, :, :].rearrange("p t (d j) -> p j d t", j=4), scalar1=1.0, scalar2=0.0, op0=ALU.mult, op1=ALU.add
                )
                wis.append(wi)

        def quant_w():
            for g in range(2):
                wc = keep.tile([P, 4 * P], U32, align_bytes=64, name=f"w_codes_{g}")
                ws = keep.tile([P, 4 * P], U8, align_bytes=64, name=f"w_scales_{g}")
                nc.vector.quantize_mx(out=wc[:].bitcast(E4M3), scales=ws[:], in_=wis[g][:].rearrange("p j d t -> p (j d t)"))
                w_codes.append(wc)
                w_scales.append(ws)

        acc2s = {}

        def mm2_pass(a, h, d, g):
            if g == 0:
                acc2s[a, h, d] = psum.tile([P, NH], F32, name="acc2", tag="bank")
            nc.tensor.matmul_mx(
                out=acc2s[a, h, d][:],
                lhsT=w_codes[g][:, P * d : P * (d + 1)].bitcast(E4M3),
                lhsT_scale=w_scales[g][:, P * d : P * (d + 1)],
                rhs=h_codes[a, g, h][:].bitcast(E5M2),
                rhs_scale=h_scales[a, g, h][:],
                start=(g == 0),
                stop=(g == 1),
            )

        def finish(a, h, d, eng):
            res = work.tile([P, NH], F32, align_bytes=64, name="res", bufs=6)
            if eng == "V":
                nc.vector.tensor_scalar(out=res[:], in0=acc2s[a, h, d][:], scalar1=b_sb[:, d : d + 1], scalar2=None, op0=ALU.add)
            else:
                nc.scalar.activation(out=res[:], in_=acc2s[a, h, d][:], func=ACT.Identity, bias=b_sb[:, d : d + 1], scale=1.0)
            nc.sync.dma_start(out=out[a].rearrange("(p j) m -> p j m", j=4)[:, d, NH * h : NH * (h + 1)], in_=res[:])

        def mm2(a, h, d, eng="S"):
            mm2_pass(a, h, d, 0)
            mm2_pass(a, h, d, 1)
            later("OUT", 0, lambda: finish(a, h, d, eng))

        for n in range(4):
            x_bank(0, 0, n)
            tick()
        nc.vector.tensor_copy(out=gain_sb[:], in_=gain_bf[:])
        xq = [(a, g, n) for a, g in ((0, 1), (1, 0), (1, 1)) for n in range(6)]
        mm1(0, 0)
        tick()
        for n in range(4, 6):
            x_bank(0, 0, n)
            tick()
        for i in range(8):
            for t in range(4):
                if (i, t) != (0, 0):
                    mm1(i, t)
                    tick()
                if clock["slot"] >= pr["wslot"] and not wis:
                    prep_w()
                for k in range(pr["xrun"].get((i, t), 0)):
                    if xq:
                        x_bank(*xq.pop(0))
                        tick()
                for m in pr["mm2"].get((i, t), ()):
                    if not w_codes:
                        quant_w()
                    mm2(*m)
                    tick()
        def flush():
            while pending:
                tick()
        for m in pr["tailplan"]:
            if m[0] == "f":
                mm2(1, 0, m[1], m[2])
                tick()
            elif m[0] == "p":
                mm2_pass(1, 1, m[1], 0)
            elif m[0] == "w":
                flush()
            else:
                mm2_pass(1, 1, m[1], 1)
                finish(1, 1, m[1], m[2])
        flush()
